import numpy as np, ml_dtypes
CORES = [242,247,114,119]
N = 4
import mx_ref
BF = ml_dtypes.bfloat16
def entries(a):
    return np.ascontiguousarray(a.T).reshape(-1)
def table(e):
    return np.ascontiguousarray(np.reshape(e, (-1, 16)).T).astype(np.int32)
def cols(t, e):
    v = np.concatenate([t.reshape(128, -1, 4), np.zeros((128, 1, 4), BF)], axis=1)
    return np.ascontiguousarray(v[:, e]).reshape(128, -1)
def tile(rs):
    return np.stack(rs, axis=2).reshape(128, -1).astype(BF)
def cut(t, i, w=512):
    return t[:, w * i:w * i + w]
def f(rng, *shape):
    return mx_ref.flush((rng.standard_normal(shape, dtype=np.float32) * np.exp2(rng.integers(-2, 3, shape[:-1] + (1,)))).astype(BF))
def wide(rng, *shape, cols=0):
    v = rng.standard_normal(shape, dtype=np.float32) * np.exp2(rng.integers(-12, 13, shape)).astype(np.float32)
    if cols: v *= np.repeat(np.exp2(rng.integers(-cols, cols + 1, shape[:-2] + (1, shape[-1] // 4))) * (rng.random(shape[:-2] + (1, shape[-1] // 4)) > 0.0625), 4, axis=-1).astype(np.float32)
    return mx_ref.flush(v.astype(BF))
T, P, CAPP = 128, 128, 32
BASE = T + 3 * P
def sends(a):
    return entries(a).reshape(3, N, CAPP)
def filled(s, r, t):
    return s[:, :t, r].transpose(1, 0, 2).reshape(-1) >= 0
def lists(rng, how=""):
    s = np.full((N, 3, N, CAPP), -1)
    a = int(rng.integers(0, N)); same = (a, int(rng.integers(0, 3)), (a + int(rng.integers(1, N))) % N)
    for t in range(3):
        for q in range(N):
            got = BASE + np.flatnonzero(filled(s, q, t))
            for r in range(N):
                if q == r: continue
                least = 1 if t == 0 and r == (q + 1) % N else 0
                k = rng.permutation(CAPP)[:CAPP if how == "far" else rng.integers(least, CAPP + 1)]
                e = rng.integers(T + (t - 1) * P if how == "far" and t > 0 else 0, T + t * P, len(k))
                if t > 0:
                    m = (len(k) + 1) // 2; e[:m] = got[rng.integers(0, len(got), m)]
                s[q, t, r, k] = e
                if how == "shared" and (q, t, r) == same: s[q, t, r] = rng.integers(0, T + t * P)
    c = np.zeros((N, 2, 3, P), int)
    for r in range(N):
        for t in range(3):
            low = 2 if how == "skip" and t == 2 else t + 1
            own = T + (low - 1) * P; got = BASE + np.flatnonzero(filled(s, r, low))
            for h in range(2):
                c[r, h, t] = rng.integers(0, own, P)
                if len(got):
                    there = np.ones(P, bool) if how == "far" else rng.random(P) < 0.5
                    c[r, h, t] = np.where(there, got[rng.integers(0, len(got), P)], c[r, h, t])
            if how == "shared":
                one = int(c[r, 0, t, 0]); k = rng.permutation(P)
                c[r, 0, t, k[:P - P // 8]] = one; c[r, 1, t, k[:P // 8]] = one
            if how == "chains":
                c[r, 0, t] = np.arange(P) % T if t == 0 else T + (t - 1) * P + np.arange(P)
                c[r, 1, t] = rng.integers(0, T, P)
    return {"sn": np.stack([table(s[r]) for r in range(N)]), "lc": np.stack([table(c[r, 0]) for r in range(N)]), "rc": np.stack([table(c[r, 1]) for r in range(N)])}
def setup_inputs(rng):
    return {"x": f(rng, N, 128, 4 * T), "wl": np.stack([f(rng, 128, 2048)] * N), "wr": np.stack([f(rng, 128, 2048)] * N), "v": f(rng, N, 128, 512), **lists(rng)}
def setup_inputs_chains(rng):
    return {**setup_inputs(rng), **lists(rng, "chains")}
def setup_inputs_far(rng):
    return {**setup_inputs(rng), **lists(rng, "far")}
def setup_inputs_shared(rng):
    return {**setup_inputs(rng), **lists(rng, "shared")}
def setup_inputs_skip(rng):
    return {**setup_inputs(rng), **lists(rng, "skip")}
def setup_inputs_spread(rng):
    d = setup_inputs(rng); d["x"] = wide(rng, N, 128, 4 * T, cols=8); return d
def check_inputs(d):
    b = []
    for n in ("wl", "wr"):
        if any((d[n][r] != d[n][0]).any() for r in range(N)): b.append(n)
    s = np.stack([sends(d["sn"][r]) for r in range(N)])
    for r in range(N):
        for t in range(3):
            own = np.concatenate([np.ones(T + t * P, bool), np.zeros((3 - t) * P, bool)])
            ok = np.concatenate([own, filled(s, r, t)]); e = s[r, t]
            if e.min() < -1 or e.max() >= len(ok) or not ok[e[e >= 0]].all() or (s[r, t, r] != -1).any(): b.append("sn")
            ok = np.concatenate([own, filled(s, r, t + 1)])
            for n in ("lc", "rc"):
                e = entries(d[n][r])[t * P:t * P + P]
                if e.min() < 0 or e.max() >= len(ok) or not ok[e].all(): b.append(n)
    return b
def reference(x, wl, wr, v, sn, lc, rc):
    WL = [[mx_ref.quantize(np.ascontiguousarray(cut(wl[r], i))) for i in range(4)] for r in range(N)]
    WR = [[mx_ref.quantize(np.ascontiguousarray(cut(wr[r], i))) for i in range(4)] for r in range(N)]
    pool = [x[r] for r in range(N)]; slots = [[] for r in range(N)]
    for t in range(3):
        before = [np.concatenate([pool[r], np.zeros((128, 4 * (3 - t) * P), BF)] + slots[r], axis=1) for r in range(N)]
        for r in range(N):
            for q in range(N): slots[r].append(cols(before[q], sends(sn[q])[t, r]))
        made = []
        for r in range(N):
            known = np.concatenate([before[r]] + slots[r][t * N:], axis=1)
            left = mx_ref.quantize(cols(known, entries(lc[r])[t * P:t * P + P]))
            right = mx_ref.quantize(cols(known, entries(rc[r])[t * P:t * P + P]))
            made.append(tile([np.maximum(mx_ref.matmul(WL[r][i], left) + mx_ref.matmul(WR[r][i], right), np.float32(0)) * np.float32(0.05) for i in range(4)]))
        pool = [np.concatenate([pool[r], made[r]], axis=1) for r in range(N)]
    y = np.zeros((N, 128, P), np.float32)
    for r in range(N):
        y[r] = mx_ref.matmul(mx_ref.quantize(v[r]), mx_ref.quantize(np.ascontiguousarray(pool[r][:, 4 * (T + 2 * P):])))
    return {"y": y}

@@ -1,0 +1,235 @@
+import numpy as np
+from concourse.bass import DstId, RemoteDMATransfer
+from concourse.mybir import dt, AluOpType, ActivationFunctionType
+
+NT, CAP = 128, 32
+SLOT = 4 * NT
+C05 = float(np.float32(0.05))
+F8, U8 = "float8_e4m3fn_x4", "uint8"
+WIDTH = [NT, 5 * NT, 6 * NT, 7 * NT]
+
+SCRATCH = {
+    "xt": ("sbuf", [128, 512], "bfloat16"),
+    "wlt": ("sbuf", [128, 2048], "bfloat16"),
+    "wrt": ("sbuf", [128, 2048], "bfloat16"),
+    "vt": ("sbuf", [128, 512], "bfloat16"),
+    "wlq": ("sbuf", [128, 512], F8), "wls": ("sbuf", [128, 512], U8),
+    "wrq": ("sbuf", [128, 512], F8), "wrs": ("sbuf", [128, 512], U8),
+    "vq": ("sbuf", [128, 128], F8), "vs": ("sbuf", [128, 128], U8),
+    "hq": ("sbuf", [128, 128], F8), "hs": ("sbuf", [128, 128], U8),
+    "snb": ("sbuf", [128, 24], "int32"),
+    "lcb": ("sbuf", [128, 24], "int32"),
+    "rcb": ("sbuf", [128, 24], "int32"),
+    "off1": ("sbuf", [128, 8], "uint16"),
+    "offs": ("sbuf", [128, 12], "uint16"),
+    "offl": ("sbuf", [128, 24], "uint16"),
+    "offr": ("sbuf", [128, 24], "uint16"),
+    "ip": ("sbuf", [128, 8], "int32"),
+    "ic": ("sbuf", [128, 8], "int32"),
+    "i32": ("sbuf", [128, 8], "int32"),
+    "same": ("sbuf", [128, 8], "uint16"),
+    "yb": ("sbuf", [128, 128], "float32"),
+    "ps": ("psum", [128, 512 * 5], "float32"),
+}
+for _t in range(4):
+    SCRATCH["x%d" % _t] = ("sbuf", [128, WIDTH[_t]], F8)
+    SCRATCH["p%d" % _t] = ("sbuf", [128, WIDTH[_t]], U8)
+for _t in range(1, 4):
+    SCRATCH["oq%d" % _t] = ("sbuf", [128, 128], F8)
+    SCRATCH["os%d" % _t] = ("sbuf", [128, 128], U8)
+    SCRATCH["cq%d" % _t] = ("sbuf", [128, 256], F8)
+    SCRATCH["cs%d" % _t] = ("sbuf", [128, 256], U8)
+    SCRATCH["h%d" % _t] = ("sbuf", [128, 512], "bfloat16")
+
+SEMAPHORES = ["ldx", "ldsn", "ldlr", "ldwl", "ldwr", "ldv", "stored",
+              "io1", "io2", "id1", "id2", "id3", "id4", "q0", "cv1", "cvs", "cvl", "qwl", "qwr", "qv",
+              "x1v", "x2v", "x3v", "x2s", "x3s", "mmy", "yc", "sent"]
+for _t in range(1, 4):
+    SEMAPHORES += ["%s%d" % (_n, _t) for _n in ("arrc", "arrs", "pkc", "pks", "pa", "pb", "ma", "mb", "mc", "md", "ev", "qz")]
+
+
+def lanes(T, topo, src):
+    here = set(topo.cores_of(src))
+    far = [c for c in T.cores if c not in here]
+    near = [c for c in T.cores if c in here and c != src]
+    res, used = {}, []
+    if far:
+        eng = topo.engines(src, far[0])
+        n = len(eng) // len(far)
+        for k, c in enumerate(far):
+            res[T.rank_of(c)] = eng[k * n:(k + 1) * n]
+        used = eng
+    for c in near:
+        res[T.rank_of(c)] = [e for e in topo.engines(src, c) if e not in used][::2]
+    return res
+
+
+def rank_program(g, core, T, topo):
+    rank = T.rank_of(core)
+    if rank is None:
+        return
+    S, V, A, Y, E = T.sem, g.vector, g.scalar, g.sync, g.tensor
+    COPY, RELU = ActivationFunctionType.Copy, ActivationFunctionType.Relu
+    others = [r for r in range(len(T.cores)) if r != rank]
+    lo, hi = others[0], others[-1] + 1
+    out = lanes(T, topo, core)
+    arrive = sum(len(lanes(T, topo, T.cores[r])[rank]) for r in others)
+
+    def pick_c(dst, c, src, a, b, off, e, f):
+        return V.tensor_copy(T[dst][:, c:c + 16 * (f - e)].bitcast(dt.uint32),
+                             T[src][:, a:b].bitcast(dt.uint32).indirect(T[off][:, e:f]))
+
+    def pick_s(eng, dst, c, src, a, b, off, e, f):
+        o, i = T[dst][:, c:c + 16 * (f - e)], T[src][:, a:b].indirect(T[off][:, e:f])
+        return V.tensor_copy(o, i) if eng is V else A.activation(o, i, COPY)
+
+    def place(t, d):
+        return CAP * (d - lo) if t == 1 else CAP * others.index(d)
+
+    def send(t):
+        for buf, pool, ready, arr in (("oq%d", "x%d", "pkc%d", "arrc%d"), ("os%d", "p%d", "pks%d", "arrs%d")):
+            g.wait_ge(S[ready % t], 1)
+            tr = []
+            for d in sorted(out, key=lambda r: min(out[r])):
+                rid, pid = topo.addr(T.cores[d], core)
+                a, b = place(t, d), SLOT + NT * (t - 1) + CAP * rank
+                src, dst = T[buf % t][:, a:a + CAP], T[pool % t][:, b:b + CAP]
+                if buf == "oq%d":
+                    src, dst = src.bitcast(dt.uint8), dst.bitcast(dt.uint8)
+                tr.append(RemoteDMATransfer(dst_ids=[DstId(rid=rid, pnc=pid)], dma_engine_mask=sum(1 << e for e in out[d]),
+                                            remote_sem=S[arr % t], src=src, dst=dst))
+            g.remote_dma_fused(tr, local_sem=S["sent"])
+
+    def table(q, buf, name, groups, sem):
+        for k in groups:
+            q.dma_start(T[buf][16 * k:16 * k + 16, :], T[name][:]).then_inc(S[sem], 16)
+
+    Y.dma_start(T.xt[:], T.x[:]).then_inc(S["ldx"], 16)
+    table(Y, "snb", "sn", range(4), "ldsn")
+    table(A, "snb", "sn", range(4, 8), "ldsn")
+    Y.dma_start(T.wlt[:], T.wl[:]).then_inc(S["ldwl"], 16)
+    A.dma_start(T.wrt[:], T.wr[:]).then_inc(S["ldwr"], 16)
+    table(Y, "lcb", "lc", range(8), "ldlr")
+    table(A, "rcb", "rc", range(8), "ldlr")
+    Y.dma_start(T.vt[:], T.v[:]).then_inc(S["ldv"], 16)
+
+    g.iota(T.ip[:], [[0, 8]], 0, 1).then_inc(S["io1"], 1)
+    g.iota(T.ic[:], [[16, 8]], 0, 0).then_inc(S["io2"], 1)
+    V.wait_ge(S["io1"], 1)
+    V.tensor_scalar(T.ip[:], T.ip[:], 15, None, AluOpType.bitwise_and).then_inc(S["id1"], 1)
+    V.wait_ge(S["id1"], 1)
+    V.wait_ge(S["io2"], 1)
+    V.tensor_tensor(T.i32[:], T.ip[:], T.ic[:], AluOpType.add).then_inc(S["id2"], 1)
+    V.wait_ge(S["id2"], 1)
+    V.tensor_copy(T.same[:], T.i32[:]).then_inc(S["id3"], 1)
+    V.wait_ge(S["id3"], 1)
+    V.memset(T.same[:, 2 * rank:2 * rank + 2], CAP * lo).then_inc(S["id4"], 1)
+
+    V.wait_ge(S["ldx"], 16)
+    V.quantize_mx(T.x0[:], T.p0[:], T.xt[:]).then_inc(S["q0"], 1)
+    V.wait_ge(S["ldsn"], 128)
+    V.tensor_copy(T.off1[:], T.snb[:, 0:8]).then_inc(S["cv1"], 1)
+    for q in (V, A):
+        q.wait_ge(S["q0"], 1)
+        q.wait_ge(S["cv1"], 1)
+    pick_c("oq1", 0, "x0", 0, NT, "off1", 2 * lo, 2 * hi).then_inc(S["pkc1"], 1)
+    pick_s(A, "os1", 0, "p0", 0, NT, "off1", 2 * lo, 2 * hi).then_inc(S["pks1"], 1)
+    send(1)
+
+    for t in range(1, 4):
+        V.quantize_mx(T["x%d" % t][:, 0:NT], T["p%d" % t][:, 0:NT], T.xt[:]).then_inc(S["x%dv" % t], 1)
+    runs = [(a, b) for a, b in ((0, rank), (rank + 1, len(T.cores))) if b > a]
+    for t in (2, 3):
+        at = 6 * (t - 2)
+        for a, b in runs:
+            V.tensor_copy(T.offs[:, at:at + 2 * (b - a)], T.snb[:, 8 * (t - 1) + 2 * a:8 * (t - 1) + 2 * b]).then_inc(S["cvs"], 1)
+            at += 2 * (b - a)
+    V.wait_ge(S["ldwl"], 16)
+    V.quantize_mx(T.wlq[:], T.wls[:], T.wlt[:]).then_inc(S["qwl"], 1)
+    V.wait_ge(S["ldwr"], 16)
+    V.quantize_mx(T.wrq[:], T.wrs[:], T.wrt[:]).then_inc(S["qwr"], 1)
+    V.wait_ge(S["ldlr"], 256)
+    V.tensor_copy(T.offl[:], T.lcb[:]).then_inc(S["cvl"], 1)
+    V.tensor_copy(T.offr[:], T.rcb[:]).then_inc(S["cvl"], 1)
+    for q in (V, A):
+        q.wait_ge(S["cvl"], 2)
+        q.wait_ge(S["id4"], 1)
+        q.wait_ge(S["cvs"], 2 * len(runs))
+
+    for t in range(1, 4):
+        x, p, cq, cs, h = "x%d" % t, "p%d" % t, "cq%d" % t, "cs%d" % t, T["h%d" % t]
+        wide, c = WIDTH[t], 8 * (t - 1)
+        pa, pb = S["pa%d" % t], S["pb%d" % t]
+        mm = [S["m%s%d" % (k, t)] for k in "abcd"]
+        ev, qz = S["ev%d" % t], S["qz%d" % t]
+        ready = [1, 3, 5][t - 1]
+        V.wait_ge(S["x%dv" % t], ready)
+        V.wait_ge(S["arrc%d" % t], arrive)
+        pick_c(cq, 0, x, 0, wide, "offl", c, c + 4).then_inc(pa, 1)
+        pick_c(cq, 64, x, 0, wide, "offl", c + 4, c + 8).then_inc(pa, 1)
+        pick_c(cq, NT, x, 0, wide, "offr", c, c + 8).then_inc(pb, 1)
+        A.wait_ge(S["x%dv" % t], ready)
+        for q in (V, A):
+            if t > 1:
+                q.wait_ge(S["x%ds" % t], t - 1)
+            q.wait_ge(S["arrs%d" % t], arrive)
+        pick_s(V, cs, 0, p, 0, wide, "offl", c, c + 4).then_inc(pa, 1)
+        pick_s(A, cs, 64, p, 0, wide, "offl", c + 4, c + 8).then_inc(pa, 1)
+        pick_s(A, cs, NT, p, 0, wide, "offr", c, c + 8).then_inc(pb, 1)
+
+        def left(i):
+            E.matmul_mx(T.ps[:, 512 * i:512 * i + NT], T.wlq[:, NT * i:NT * i + NT], T.wls[:, NT * i:NT * i + NT],
+                        T[cq][:, 0:NT], T[cs][:, 0:NT], True, False)
+
+        def right(i):
+            E.matmul_mx(T.ps[:, 512 * i:512 * i + NT], T.wrq[:, NT * i:NT * i + NT], T.wrs[:, NT * i:NT * i + NT],
+                        T[cq][:, NT:2 * NT], T[cs][:, NT:2 * NT], False, True).then_inc(mm[i], 1)
+
+        if t == 1:
+            E.wait_ge(S["qwl"], 1)
+            E.wait_ge(S["qwr"], 1)
+        E.wait_ge(pa, 4)
+        left(0)
+        left(1)
+        left(2)
+        E.wait_ge(pb, 2)
+        right(0)
+        left(3)
+        right(1)
+        right(2)
+        right(3)
+        for i in (0, 2):
+            A.wait_ge(mm[i], 1)
+            A.activation(h[:, i:512:4], T.ps[:, 512 * i:512 * i + NT], RELU, scale=C05).then_inc(ev, 1)
+        for i in (1, 3):
+            V.wait_ge(mm[i], 1)
+            V.tensor_scalar(h[:, i:512:4], T.ps[:, 512 * i:512 * i + NT], 0.0, C05, AluOpType.max, AluOpType.mult).then_inc(ev, 1)
+        V.wait_ge(ev, 4)
+        if t == 3:
+            V.quantize_mx(T.hq[:], T.hs[:], h[:]).then_inc(qz, 1)
+            break
+        V.quantize_mx(T[x][:, NT * t:NT * t + NT], T[p][:, NT * t:NT * t + NT], h[:]).then_inc(qz, 1)
+        s = 6 * (t - 1)
+        V.wait_ge(qz, 1)
+        A.wait_ge(qz, 1)
+        pick_c("oq%d" % (t + 1), 0, x, 0, wide, "offs", s, s + 6).then_inc(S["pkc%d" % (t + 1)], 1)
+        pick_s(A, "os%d" % (t + 1), 0, p, 0, wide, "offs", s, s + 6).then_inc(S["pks%d" % (t + 1)], 1)
+        send(t + 1)
+        b = SLOT + NT * (t - 1)
+        for n in range(t + 1, 4):
+            V.quantize_mx(T["x%d" % n][:, NT * t:NT * t + NT], T["p%d" % n][:, NT * t:NT * t + NT], h[:]).then_inc(S["x%dv" % n], 1)
+            pick_c("x%d" % n, b, x, b, b + NT, "same", 0, 8).then_inc(S["x%dv" % n], 1)
+            pick_s(A, "p%d" % n, b, p, b, b + NT, "same", 0, 8).then_inc(S["x%ds" % n], 1)
+        if t == 1:
+            V.wait_ge(S["ldv"], 16)
+            V.quantize_mx(T.vq[:], T.vs[:], T.vt[:]).then_inc(S["qv"], 1)
+
+    E.wait_ge(S["qv"], 1)
+    E.wait_ge(S["qz3"], 1)
+    E.matmul_mx(T.ps[:, 2048:2048 + NT], T.vq[:], T.vs[:], T.hq[:], T.hs[:], True, True).then_inc(S["mmy"], 1)
+    V.wait_ge(S["mmy"], 1)
+    V.tensor_copy(T.yb[:], T.ps[:, 2048:2048 + NT]).then_inc(S["yc"], 1)
+    Y.wait_ge(S["yc"], 1)
+    Y.dma_start(T.y[:], T.yb[:]).then_inc(S["stored"], 16)
+    Y.wait_ge(S["stored"], 16)
+    g.wait_ge(S["sent"], 6 * sum(len(e) for e in out.values()))

@@ -20,8 +20,7 @@ SCRATCH = {
     "snb": ("sbuf", [128, 24], "int32"),
     "lcb": ("sbuf", [128, 24], "int32"),
     "rcb": ("sbuf", [128, 24], "int32"),
-    "off1": ("sbuf", [128, 8], "uint16"),
-    "offs": ("sbuf", [128, 12], "uint16"),
+    "offs": ("sbuf", [128, 24], "uint16"),
     "offl": ("sbuf", [128, 24], "uint16"),
     "offr": ("sbuf", [128, 24], "uint16"),
     "ip": ("sbuf", [128, 8], "int32"),
@@ -45,7 +44,7 @@ SEMAPHORES = ["ldx", "ldsn", "ldlr", "ldwl", "ldwr", "ldv", "stored",
               "io1", "io2", "id1", "id2", "id3", "id4", "q0", "cv1", "cvs", "cvl", "qwl", "qwr", "qv",
               "x1v", "x2v", "x3v", "x2s", "x3s", "mmy", "yc", "sent"]
 for _t in range(1, 4):
-    SEMAPHORES += ["%s%d" % (_n, _t) for _n in ("arrc", "arrs", "pkc", "pks", "pa", "pb", "ma", "mb", "mc", "md", "ev", "qz")]
+    SEMAPHORES += ["%s%d" % (_n, _t) for _n in ("arrc", "arrs", "pkc", "pkd", "pke", "psc", "psd", "pse", "pa", "pb", "ma", "mb", "mc", "md", "ev", "qz")]
 
 
 def lanes(T, topo, src):
@@ -60,8 +59,19 @@ def lanes(T, topo, src):
             res[T.rank_of(c)] = eng[k * n:(k + 1) * n]
         used = eng
     for c in near:
-        res[T.rank_of(c)] = [e for e in topo.engines(src, c) if e not in used][::2]
+        res[T.rank_of(c)] = [e for e in topo.engines(src, c) if e not in used]
     return res
+
+
+def calls(T, topo, src, t):
+    out = lanes(T, topo, src)
+    near = [r for r in out if T.cores[r] in topo.cores_of(src)]
+    first, last = sorted((r for r in out if r not in near), key=lambda r: topo.die(T.cores[r]) == topo.die(src))
+    every = sorted(out[first] + out[last])
+    wide = {r: every if t > 1 else out[r] for r in (first, last)}
+    return [("c", "pkc%d", 1, {first: wide[first]}), ("c", "pkd%d", 1, {last: wide[last]}),
+            ("s", "psc%d", 1, {first: wide[first]}), ("s", "psd%d", 1, {last: wide[last]}),
+            ("c", "pke%d", 1, {near[0]: out[near[0]]}), ("s", "pse%d", 1, {near[0]: out[near[0]]})]
 
 
 def rank_program(g, core, T, topo):
@@ -71,9 +81,11 @@ def rank_program(g, core, T, topo):
     S, V, A, Y, E = T.sem, g.vector, g.scalar, g.sync, g.tensor
     COPY, RELU = ActivationFunctionType.Copy, ActivationFunctionType.Relu
     others = [r for r in range(len(T.cores)) if r != rank]
-    lo, hi = others[0], others[-1] + 1
-    out = lanes(T, topo, core)
-    arrive = sum(len(lanes(T, topo, T.cores[r])[rank]) for r in others)
+    lo = others[0]
+    order = others
+    plan = {t: calls(T, topo, core, t) for t in (1, 2, 3)}
+    arrive = {(k, t): sum(len(call.get(rank, [])) for r in others for kind, _, _, call in calls(T, topo, T.cores[r], t) if kind == k)
+              for k in "cs" for t in (1, 2, 3)}
 
     def pick_c(dst, c, src, a, b, off, e, f):
         return V.tensor_copy(T[dst][:, c:c + 16 * (f - e)].bitcast(dt.uint32),
@@ -83,35 +95,50 @@ def rank_program(g, core, T, topo):
         o, i = T[dst][:, c:c + 16 * (f - e)], T[src][:, a:b].indirect(T[off][:, e:f])
         return V.tensor_copy(o, i) if eng is V else A.activation(o, i, COPY)
 
-    def place(t, d):
-        return CAP * (d - lo) if t == 1 else CAP * others.index(d)
+    def place(d):
+        return CAP * order.index(d)
 
     def send(t):
-        for buf, pool, ready, arr in (("oq%d", "x%d", "pkc%d", "arrc%d"), ("os%d", "p%d", "pks%d", "arrs%d")):
-            g.wait_ge(S[ready % t], 1)
+        for kind, ready, n, call in plan[t]:
+            buf, pool, arr = ("oq%d", "x%d", "arrc%d") if kind == "c" else ("os%d", "p%d", "arrs%d")
+            g.wait_ge(S[ready % t], n)
             tr = []
-            for d in sorted(out, key=lambda r: min(out[r])):
+            for d in sorted(call, key=lambda r: min(call[r])):
                 rid, pid = topo.addr(T.cores[d], core)
-                a, b = place(t, d), SLOT + NT * (t - 1) + CAP * rank
+                a, b = place(d), SLOT + NT * (t - 1) + CAP * rank
                 src, dst = T[buf % t][:, a:a + CAP], T[pool % t][:, b:b + CAP]
-                if buf == "oq%d":
+                if kind == "c":
                     src, dst = src.bitcast(dt.uint8), dst.bitcast(dt.uint8)
-                tr.append(RemoteDMATransfer(dst_ids=[DstId(rid=rid, pnc=pid)], dma_engine_mask=sum(1 << e for e in out[d]),
+                tr.append(RemoteDMATransfer(dst_ids=[DstId(rid=rid, pnc=pid)], dma_engine_mask=sum(1 << e for e in call[d]),
                                             remote_sem=S[arr % t], src=src, dst=dst))
             g.remote_dma_fused(tr, local_sem=S["sent"])
+
+    def pick_out(t, x, p, wide):
+        s = 8 * (t - 1)
+        for kind, ready, _, call in plan[t]:
+            if kind == "c":
+                a = min(order.index(d) for d in call)
+                e, f = s + 2 * min(call), s + 2 * (min(call) + len(call))
+                pick_c("oq%d" % t, CAP * a, x, 0, wide, "offs", e, f).then_inc(S[ready % t], 1)
+                pick_s(A, "os%d" % t, CAP * a, p, 0, wide, "offs", e, f).then_inc(S[ready.replace("pk", "ps") % t], 1)
+        send(t)
 
     def table(q, buf, name, groups, sem):
         for k in groups:
             q.dma_start(T[buf][16 * k:16 * k + 16, :], T[name][:]).then_inc(S[sem], 16)
 
     Y.dma_start(T.xt[:], T.x[:]).then_inc(S["ldx"], 16)
-    table(Y, "snb", "sn", range(4), "ldsn")
-    table(A, "snb", "sn", range(4, 8), "ldsn")
+    table(A, "snb", "sn", range(4), "ldsn")
+    table(Y, "lcb", "lc", range(4), "ldlr")
     Y.dma_start(T.wlt[:], T.wl[:]).then_inc(S["ldwl"], 16)
+    table(A, "rcb", "rc", range(4), "ldlr")
     A.dma_start(T.wrt[:], T.wr[:]).then_inc(S["ldwr"], 16)
-    table(Y, "lcb", "lc", range(8), "ldlr")
-    table(A, "rcb", "rc", range(8), "ldlr")
+    Y.wait_ge(S["arrs1"], arrive["s", 1])
     Y.dma_start(T.vt[:], T.v[:]).then_inc(S["ldv"], 16)
+
+    def offsets(dst, c, src, a, b, sem):
+        for half in (0, 64):
+            V.tensor_copy(T[dst][half:half + 64, c:c + b - a], T[src][0:64, a:b]).then_inc(S[sem], 1)
 
     g.iota(T.ip[:], [[0, 8]], 0, 1).then_inc(S["io1"], 1)
     g.iota(T.ic[:], [[16, 8]], 0, 0).then_inc(S["io2"], 1)
@@ -120,41 +147,32 @@ def rank_program(g, core, T, topo):
     V.wait_ge(S["id1"], 1)
     V.wait_ge(S["io2"], 1)
     V.tensor_tensor(T.i32[:], T.ip[:], T.ic[:], AluOpType.add).then_inc(S["id2"], 1)
-    V.wait_ge(S["id2"], 1)
-    V.tensor_copy(T.same[:], T.i32[:]).then_inc(S["id3"], 1)
-    V.wait_ge(S["id3"], 1)
-    V.memset(T.same[:, 2 * rank:2 * rank + 2], CAP * lo).then_inc(S["id4"], 1)
 
+    V.wait_ge(S["ldsn"], 64)
+    offsets("offs", 0, "snb", 0, 24, "cv1")
     V.wait_ge(S["ldx"], 16)
     V.quantize_mx(T.x0[:], T.p0[:], T.xt[:]).then_inc(S["q0"], 1)
-    V.wait_ge(S["ldsn"], 128)
-    V.tensor_copy(T.off1[:], T.snb[:, 0:8]).then_inc(S["cv1"], 1)
     for q in (V, A):
+        q.wait_ge(S["cv1"], 2)
         q.wait_ge(S["q0"], 1)
-        q.wait_ge(S["cv1"], 1)
-    pick_c("oq1", 0, "x0", 0, NT, "off1", 2 * lo, 2 * hi).then_inc(S["pkc1"], 1)
-    pick_s(A, "os1", 0, "p0", 0, NT, "off1", 2 * lo, 2 * hi).then_inc(S["pks1"], 1)
-    send(1)
+    pick_out(1, "x0", "p0", NT)
 
+    V.wait_ge(S["id2"], 1)
+    V.tensor_copy(T.same[:], T.i32[:]).then_inc(S["id3"], 1)
     for t in range(1, 4):
         V.quantize_mx(T["x%d" % t][:, 0:NT], T["p%d" % t][:, 0:NT], T.xt[:]).then_inc(S["x%dv" % t], 1)
-    runs = [(a, b) for a, b in ((0, rank), (rank + 1, len(T.cores))) if b > a]
-    for t in (2, 3):
-        at = 6 * (t - 2)
-        for a, b in runs:
-            V.tensor_copy(T.offs[:, at:at + 2 * (b - a)], T.snb[:, 8 * (t - 1) + 2 * a:8 * (t - 1) + 2 * b]).then_inc(S["cvs"], 1)
-            at += 2 * (b - a)
+    V.wait_ge(S["id3"], 1)
+    V.memset(T.same[:, 2 * rank:2 * rank + 2], CAP * lo).then_inc(S["id4"], 1)
+    V.wait_ge(S["ldlr"], 128)
+    offsets("offl", 0, "lcb", 0, 24, "cvl")
+    offsets("offr", 0, "rcb", 0, 24, "cvl")
     V.wait_ge(S["ldwl"], 16)
     V.quantize_mx(T.wlq[:], T.wls[:], T.wlt[:]).then_inc(S["qwl"], 1)
     V.wait_ge(S["ldwr"], 16)
     V.quantize_mx(T.wrq[:], T.wrs[:], T.wrt[:]).then_inc(S["qwr"], 1)
-    V.wait_ge(S["ldlr"], 256)
-    V.tensor_copy(T.offl[:], T.lcb[:]).then_inc(S["cvl"], 1)
-    V.tensor_copy(T.offr[:], T.rcb[:]).then_inc(S["cvl"], 1)
     for q in (V, A):
-        q.wait_ge(S["cvl"], 2)
+        q.wait_ge(S["cvl"], 4)
         q.wait_ge(S["id4"], 1)
-        q.wait_ge(S["cvs"], 2 * len(runs))
 
     for t in range(1, 4):
         x, p, cq, cs, h = "x%d" % t, "p%d" % t, "cq%d" % t, "cs%d" % t, T["h%d" % t]
@@ -164,17 +182,17 @@ def rank_program(g, core, T, topo):
         ev, qz = S["ev%d" % t], S["qz%d" % t]
         ready = [1, 3, 5][t - 1]
         V.wait_ge(S["x%dv" % t], ready)
-        V.wait_ge(S["arrc%d" % t], arrive)
+        V.wait_ge(S["arrc%d" % t], arrive["c", t])
         pick_c(cq, 0, x, 0, wide, "offl", c, c + 4).then_inc(pa, 1)
         pick_c(cq, 64, x, 0, wide, "offl", c + 4, c + 8).then_inc(pa, 1)
-        pick_c(cq, NT, x, 0, wide, "offr", c, c + 8).then_inc(pb, 1)
         A.wait_ge(S["x%dv" % t], ready)
         for q in (V, A):
             if t > 1:
                 q.wait_ge(S["x%ds" % t], t - 1)
-            q.wait_ge(S["arrs%d" % t], arrive)
+            q.wait_ge(S["arrs%d" % t], arrive["s", t])
         pick_s(V, cs, 0, p, 0, wide, "offl", c, c + 4).then_inc(pa, 1)
         pick_s(A, cs, 64, p, 0, wide, "offl", c + 4, c + 8).then_inc(pa, 1)
+        pick_c(cq, NT, x, 0, wide, "offr", c, c + 8).then_inc(pb, 1)
         pick_s(A, cs, NT, p, 0, wide, "offr", c, c + 8).then_inc(pb, 1)
 
         def left(i):
@@ -187,17 +205,14 @@ def rank_program(g, core, T, topo):
 
         if t == 1:
             E.wait_ge(S["qwl"], 1)
-            E.wait_ge(S["qwr"], 1)
         E.wait_ge(pa, 4)
-        left(0)
-        left(1)
-        left(2)
+        for i in range(4):
+            left(i)
+        if t == 1:
+            E.wait_ge(S["qwr"], 1)
         E.wait_ge(pb, 2)
-        right(0)
-        left(3)
-        right(1)
-        right(2)
-        right(3)
+        for i in range(4):
+            right(i)
         for i in (0, 2):
             A.wait_ge(mm[i], 1)
             A.activation(h[:, i:512:4], T.ps[:, 512 * i:512 * i + NT], RELU, scale=C05).then_inc(ev, 1)
@@ -209,12 +224,9 @@ def rank_program(g, core, T, topo):
             V.quantize_mx(T.hq[:], T.hs[:], h[:]).then_inc(qz, 1)
             break
         V.quantize_mx(T[x][:, NT * t:NT * t + NT], T[p][:, NT * t:NT * t + NT], h[:]).then_inc(qz, 1)
-        s = 6 * (t - 1)
         V.wait_ge(qz, 1)
         A.wait_ge(qz, 1)
-        pick_c("oq%d" % (t + 1), 0, x, 0, wide, "offs", s, s + 6).then_inc(S["pkc%d" % (t + 1)], 1)
-        pick_s(A, "os%d" % (t + 1), 0, p, 0, wide, "offs", s, s + 6).then_inc(S["pks%d" % (t + 1)], 1)
-        send(t + 1)
+        pick_out(t + 1, x, p, wide)
         b = SLOT + NT * (t - 1)
         for n in range(t + 1, 4):
             V.quantize_mx(T["x%d" % n][:, NT * t:NT * t + NT], T["p%d" % n][:, NT * t:NT * t + NT], h[:]).then_inc(S["x%dv" % n], 1)
@@ -232,4 +244,4 @@ def rank_program(g, core, T, topo):
     Y.wait_ge(S["yc"], 1)
     Y.dma_start(T.y[:], T.yb[:]).then_inc(S["stored"], 16)
     Y.wait_ge(S["stored"], 16)
-    g.wait_ge(S["sent"], 6 * sum(len(e) for e in out.values()))
+    g.wait_ge(S["sent"], sum(len(e) for t in plan for _, _, _, call in plan[t] for e in call.values()))

import numpy as np
from concourse.bass import DstId, RemoteDMATransfer
from concourse.mybir import dt, AluOpType, ActivationFunctionType

NT, CAP = 128, 32
SLOT = 4 * NT
C05 = float(np.float32(0.05))
F8, U8 = "float8_e4m3fn_x4", "uint8"
WIDTH = [NT, 5 * NT, 6 * NT, 7 * NT]

SCRATCH = {
    "xt": ("sbuf", [128, 512], "bfloat16"),
    "wlt": ("sbuf", [128, 2048], "bfloat16"),
    "wrt": ("sbuf", [128, 2048], "bfloat16"),
    "vt": ("sbuf", [128, 512], "bfloat16"),
    "wlq": ("sbuf", [128, 512], F8), "wls": ("sbuf", [128, 512], U8),
    "wrq": ("sbuf", [128, 512], F8), "wrs": ("sbuf", [128, 512], U8),
    "vq": ("sbuf", [128, 128], F8), "vs": ("sbuf", [128, 128], U8),
    "hq": ("sbuf", [128, 128], F8), "hs": ("sbuf", [128, 128], U8),
    "snb": ("sbuf", [128, 24], "int32"),
    "lcb": ("sbuf", [128, 24], "int32"),
    "rcb": ("sbuf", [128, 24], "int32"),
    "offs": ("sbuf", [128, 24], "uint16"),
    "offl": ("sbuf", [128, 24], "uint16"),
    "offr": ("sbuf", [128, 24], "uint16"),
    "ip": ("sbuf", [128, 8], "int32"),
    "ic": ("sbuf", [128, 8], "int32"),
    "i32": ("sbuf", [128, 8], "int32"),
    "same": ("sbuf", [128, 8], "uint16"),
    "yb": ("sbuf", [128, 128], "float32"),
    "ps": ("psum", [128, 512 * 5], "float32"),
}
for _t in range(4):
    SCRATCH["x%d" % _t] = ("sbuf", [128, WIDTH[_t]], F8)
    SCRATCH["p%d" % _t] = ("sbuf", [128, WIDTH[_t]], U8)
for _t in range(1, 4):
    SCRATCH["oq%d" % _t] = ("sbuf", [128, 128], F8)
    SCRATCH["os%d" % _t] = ("sbuf", [128, 128], U8)
    SCRATCH["cq%d" % _t] = ("sbuf", [128, 256], F8)
    SCRATCH["cs%d" % _t] = ("sbuf", [128, 256], U8)
    SCRATCH["h%d" % _t] = ("sbuf", [128, 512], "bfloat16")

SEMAPHORES = ["ldx", "ldsn", "ldlr", "ldwl", "ldwr", "ldv", "stored",
              "io1", "io2", "id1", "id2", "id3", "id4", "q0", "cv1", "cvs", "cvl", "qwl", "qwr", "qv",
              "x1v", "x2v", "x3v", "x2s", "x3s", "mmy", "yc", "sent"]
for _t in range(1, 4):
    SEMAPHORES += ["%s%d" % (_n, _t) for _n in ("arrc", "arrs", "pkc", "pkd", "pke", "psc", "psd", "pse", "pa", "pb", "ma", "mb", "mc", "md", "ev", "qz")]


def lanes(T, topo, src):
    here = set(topo.cores_of(src))
    far = [c for c in T.cores if c not in here]
    near = [c for c in T.cores if c in here and c != src]
    res, used = {}, []
    if far:
        eng = topo.engines(src, far[0])
        n = len(eng) // len(far)
        for k, c in enumerate(far):
            res[T.rank_of(c)] = eng[k * n:(k + 1) * n]
        used = eng
    for c in near:
        res[T.rank_of(c)] = [e for e in topo.engines(src, c) if e not in used]
    return res


def calls(T, topo, src, t):
    out = lanes(T, topo, src)
    near = [r for r in out if T.cores[r] in topo.cores_of(src)]
    first, last = sorted((r for r in out if r not in near), key=lambda r: topo.die(T.cores[r]) == topo.die(src))
    every = sorted(out[first] + out[last])
    wide = {r: every if t > 1 else out[r] for r in (first, last)}
    return [("c", "pkc%d", 1, {first: wide[first]}), ("c", "pkd%d", 1, {last: wide[last]}),
            ("s", "psc%d", 1, {first: wide[first]}), ("s", "psd%d", 1, {last: wide[last]}),
            ("c", "pke%d", 1, {near[0]: out[near[0]]}), ("s", "pse%d", 1, {near[0]: out[near[0]]})]


def rank_program(g, core, T, topo):
    rank = T.rank_of(core)
    if rank is None:
        return
    S, V, A, Y, E = T.sem, g.vector, g.scalar, g.sync, g.tensor
    COPY, RELU = ActivationFunctionType.Copy, ActivationFunctionType.Relu
    others = [r for r in range(len(T.cores)) if r != rank]
    lo = others[0]
    order = others
    plan = {t: calls(T, topo, core, t) for t in (1, 2, 3)}
    arrive = {(k, t): sum(len(call.get(rank, [])) for r in others for kind, _, _, call in calls(T, topo, T.cores[r], t) if kind == k)
              for k in "cs" for t in (1, 2, 3)}

    def pick_c(dst, c, src, a, b, off, e, f):
        return V.tensor_copy(T[dst][:, c:c + 16 * (f - e)].bitcast(dt.uint32),
                             T[src][:, a:b].bitcast(dt.uint32).indirect(T[off][:, e:f]))

    def pick_s(eng, dst, c, src, a, b, off, e, f):
        o, i = T[dst][:, c:c + 16 * (f - e)], T[src][:, a:b].indirect(T[off][:, e:f])
        return V.tensor_copy(o, i) if eng is V else A.activation(o, i, COPY)

    def place(d):
        return CAP * order.index(d)

    def send(t):
        for kind, ready, n, call in plan[t]:
            buf, pool, arr = ("oq%d", "x%d", "arrc%d") if kind == "c" else ("os%d", "p%d", "arrs%d")
            g.wait_ge(S[ready % t], n)
            tr = []
            for d in sorted(call, key=lambda r: min(call[r])):
                rid, pid = topo.addr(T.cores[d], core)
                a, b = place(d), SLOT + NT * (t - 1) + CAP * rank
                src, dst = T[buf % t][:, a:a + CAP], T[pool % t][:, b:b + CAP]
                if kind == "c":
                    src, dst = src.bitcast(dt.uint8), dst.bitcast(dt.uint8)
                tr.append(RemoteDMATransfer(dst_ids=[DstId(rid=rid, pnc=pid)], dma_engine_mask=sum(1 << e for e in call[d]),
                                            remote_sem=S[arr % t], src=src, dst=dst))
            g.remote_dma_fused(tr, local_sem=S["sent"])

    def pick_out(t, x, p, wide):
        s = 8 * (t - 1)
        for kind, ready, _, call in plan[t]:
            if kind == "c":
                a = min(order.index(d) for d in call)
                e, f = s + 2 * min(call), s + 2 * (min(call) + len(call))
                pick_c("oq%d" % t, CAP * a, x, 0, wide, "offs", e, f).then_inc(S[ready % t], 1)
                pick_s(A, "os%d" % t, CAP * a, p, 0, wide, "offs", e, f).then_inc(S[ready.replace("pk", "ps") % t], 1)
        send(t)

    def table(q, buf, name, groups, sem):
        for k in groups:
            q.dma_start(T[buf][16 * k:16 * k + 16, :], T[name][:]).then_inc(S[sem], 16)

    Y.dma_start(T.xt[:], T.x[:]).then_inc(S["ldx"], 16)
    table(A, "snb", "sn", range(4), "ldsn")
    table(Y, "lcb", "lc", range(4), "ldlr")
    Y.dma_start(T.wlt[:], T.wl[:]).then_inc(S["ldwl"], 16)
    table(A, "rcb", "rc", range(4), "ldlr")
    A.dma_start(T.wrt[:], T.wr[:]).then_inc(S["ldwr"], 16)
    Y.wait_ge(S["arrs1"], arrive["s", 1])
    Y.dma_start(T.vt[:], T.v[:]).then_inc(S["ldv"], 16)

    def offsets(dst, c, src, a, b, sem):
        for half in (0, 64):
            V.tensor_copy(T[dst][half:half + 64, c:c + b - a], T[src][0:64, a:b]).then_inc(S[sem], 1)

    g.iota(T.ip[:], [[0, 8]], 0, 1).then_inc(S["io1"], 1)
    g.iota(T.ic[:], [[16, 8]], 0, 0).then_inc(S["io2"], 1)
    V.wait_ge(S["io1"], 1)
    V.tensor_scalar(T.ip[:], T.ip[:], 15, None, AluOpType.bitwise_and).then_inc(S["id1"], 1)
    V.wait_ge(S["id1"], 1)
    V.wait_ge(S["io2"], 1)
    V.tensor_tensor(T.i32[:], T.ip[:], T.ic[:], AluOpType.add).then_inc(S["id2"], 1)

    V.wait_ge(S["ldsn"], 64)
    offsets("offs", 0, "snb", 0, 24, "cv1")
    V.wait_ge(S["ldx"], 16)
    V.quantize_mx(T.x0[:], T.p0[:], T.xt[:]).then_inc(S["q0"], 1)
    for q in (V, A):
        q.wait_ge(S["cv1"], 2)
        q.wait_ge(S["q0"], 1)
    pick_out(1, "x0", "p0", NT)

    V.wait_ge(S["id2"], 1)
    V.tensor_copy(T.same[:], T.i32[:]).then_inc(S["id3"], 1)
    for t in range(1, 4):
        V.quantize_mx(T["x%d" % t][:, 0:NT], T["p%d" % t][:, 0:NT], T.xt[:]).then_inc(S["x%dv" % t], 1)
    V.wait_ge(S["id3"], 1)
    V.memset(T.same[:, 2 * rank:2 * rank + 2], CAP * lo).then_inc(S["id4"], 1)
    V.wait_ge(S["ldlr"], 128)
    offsets("offl", 0, "lcb", 0, 24, "cvl")
    offsets("offr", 0, "rcb", 0, 24, "cvl")
    V.wait_ge(S["ldwl"], 16)
    V.quantize_mx(T.wlq[:], T.wls[:], T.wlt[:]).then_inc(S["qwl"], 1)
    V.wait_ge(S["ldwr"], 16)
    V.quantize_mx(T.wrq[:], T.wrs[:], T.wrt[:]).then_inc(S["qwr"], 1)
    for q in (V, A):
        q.wait_ge(S["cvl"], 4)
        q.wait_ge(S["id4"], 1)

    for t in range(1, 4):
        x, p, cq, cs, h = "x%d" % t, "p%d" % t, "cq%d" % t, "cs%d" % t, T["h%d" % t]
        wide, c = WIDTH[t], 8 * (t - 1)
        pa, pb = S["pa%d" % t], S["pb%d" % t]
        mm = [S["m%s%d" % (k, t)] for k in "abcd"]
        ev, qz = S["ev%d" % t], S["qz%d" % t]
        ready = [1, 3, 5][t - 1]
        V.wait_ge(S["x%dv" % t], ready)
        V.wait_ge(S["arrc%d" % t], arrive["c", t])
        pick_c(cq, 0, x, 0, wide, "offl", c, c + 4).then_inc(pa, 1)
        pick_c(cq, 64, x, 0, wide, "offl", c + 4, c + 8).then_inc(pa, 1)
        A.wait_ge(S["x%dv" % t], ready)
        for q in (V, A):
            if t > 1:
                q.wait_ge(S["x%ds" % t], t - 1)
            q.wait_ge(S["arrs%d" % t], arrive["s", t])
        pick_s(V, cs, 0, p, 0, wide, "offl", c, c + 4).then_inc(pa, 1)
        pick_s(A, cs, 64, p, 0, wide, "offl", c + 4, c + 8).then_inc(pa, 1)
        pick_c(cq, NT, x, 0, wide, "offr", c, c + 8).then_inc(pb, 1)
        pick_s(A, cs, NT, p, 0, wide, "offr", c, c + 8).then_inc(pb, 1)

        def left(i):
            E.matmul_mx(T.ps[:, 512 * i:512 * i + NT], T.wlq[:, NT * i:NT * i + NT], T.wls[:, NT * i:NT * i + NT],
                        T[cq][:, 0:NT], T[cs][:, 0:NT], True, False)

        def right(i):
            E.matmul_mx(T.ps[:, 512 * i:512 * i + NT], T.wrq[:, NT * i:NT * i + NT], T.wrs[:, NT * i:NT * i + NT],
                        T[cq][:, NT:2 * NT], T[cs][:, NT:2 * NT], False, True).then_inc(mm[i], 1)

        if t == 1:
            E.wait_ge(S["qwl"], 1)
        E.wait_ge(pa, 4)
        for i in range(4):
            left(i)
        if t == 1:
            E.wait_ge(S["qwr"], 1)
        E.wait_ge(pb, 2)
        for i in range(4):
            right(i)
        for i in (0, 2):
            A.wait_ge(mm[i], 1)
            A.activation(h[:, i:512:4], T.ps[:, 512 * i:512 * i + NT], RELU, scale=C05).then_inc(ev, 1)
        for i in (1, 3):
            V.wait_ge(mm[i], 1)
            V.tensor_scalar(h[:, i:512:4], T.ps[:, 512 * i:512 * i + NT], 0.0, C05, AluOpType.max, AluOpType.mult).then_inc(ev, 1)
        V.wait_ge(ev, 4)
        if t == 3:
            V.quantize_mx(T.hq[:], T.hs[:], h[:]).then_inc(qz, 1)
            break
        V.quantize_mx(T[x][:, NT * t:NT * t + NT], T[p][:, NT * t:NT * t + NT], h[:]).then_inc(qz, 1)
        V.wait_ge(qz, 1)
        A.wait_ge(qz, 1)
        pick_out(t + 1, x, p, wide)
        b = SLOT + NT * (t - 1)
        for n in range(t + 1, 4):
            V.quantize_mx(T["x%d" % n][:, NT * t:NT * t + NT], T["p%d" % n][:, NT * t:NT * t + NT], h[:]).then_inc(S["x%dv" % n], 1)
            pick_c("x%d" % n, b, x, b, b + NT, "same", 0, 8).then_inc(S["x%dv" % n], 1)
            pick_s(A, "p%d" % n, b, p, b, b + NT, "same", 0, 8).then_inc(S["x%ds" % n], 1)
        if t == 1:
            V.wait_ge(S["ldv"], 16)
            V.quantize_mx(T.vq[:], T.vs[:], T.vt[:]).then_inc(S["qv"], 1)

    E.wait_ge(S["qv"], 1)
    E.wait_ge(S["qz3"], 1)
    E.matmul_mx(T.ps[:, 2048:2048 + NT], T.vq[:], T.vs[:], T.hq[:], T.hs[:], True, True).then_inc(S["mmy"], 1)
    V.wait_ge(S["mmy"], 1)
    V.tensor_copy(T.yb[:], T.ps[:, 2048:2048 + NT]).then_inc(S["yc"], 1)
    Y.wait_ge(S["yc"], 1)
    Y.dma_start(T.y[:], T.yb[:]).then_inc(S["stored"], 16)
    Y.wait_ge(S["stored"], 16)
    g.wait_ge(S["sent"], sum(len(e) for t in plan for _, _, _, call in plan[t] for e in call.values()))
